import numpy as np
import ml_dtypes


def mxq(x, axis, fmt="e4m3"):
    dtype, down = {"e4m3": (ml_dtypes.float8_e4m3fn, 7), "e5m2": (ml_dtypes.float8_e5m2, 14)}[fmt]
    v = np.moveaxis(np.asarray(x, np.float32).astype(ml_dtypes.bfloat16).astype(np.float64), axis, -1)
    blocks = v.reshape(v.shape[:-1] + (-1, 32))
    amax = np.abs(blocks).max(-1, keepdims=True)
    byte = np.maximum(np.where(amax > 0, np.frexp(amax)[1] - 1 + 127, 0) - down, 1)
    scale = np.exp2(byte - 127.0)
    codes = (blocks / scale).astype(np.float32).astype(dtype).astype(np.float64)
    return np.moveaxis((codes * scale).reshape(v.shape), -1, axis)


WIDE = False


def mx_kscale(k):
    if not WIDE:
        return np.ones(k)
    levels = np.array([10, -10, 5, -5, 0])
    if k % 512:
        return np.exp2(np.random.permutation(np.resize(levels, k // 32))).repeat(32)
    a = np.empty((k // 512, 16))
    for p in range(k // 512):
        a[p, :8] = np.random.permutation(np.resize(levels, 8))
        for g in range(8):
            far = levels[np.abs(levels - a[p, g]) >= 10]
            a[p, g + 8] = far[np.random.randint(len(far))]
    return np.exp2(a.ravel()).repeat(32)


def f64(x):
    return np.asarray(x).astype(np.float64)


def striped(idx):
    return np.tile(np.asarray(idx).reshape(-1, 16).T, (8, 1)).astype(np.uint16)


def unstriped(offs):
    return offs[:16].T.reshape(-1).astype(np.int64)


E2M1 = np.array([0.0, 0.5, 1.0, 1.5, 2.0, 3.0, 4.0, 6.0, -0.0, -0.5, -1.0, -1.5, -2.0, -3.0, -4.0, -6.0])


def pack_weight(w, fmt):
    k, n = w.shape
    w = f64(np.asarray(w, np.float32).astype(ml_dtypes.bfloat16)).reshape(k // 32, 32, n)
    amax = np.abs(w).max(1)
    if fmt == "e4m3":
        byte = np.frexp(amax)[1] - 1 + 127 - 7
    else:
        mant, ex = np.frexp(amax / 6.0)
        byte = np.where(mant > 0.5, ex, ex - 1) + 127
    byte = np.clip(np.where(amax > 0, byte, 1), 1, 254)
    scaled = (w * np.exp2(127.0 - byte)[:, None, :]).reshape(k, n).astype(np.float32)
    by_word = np.ascontiguousarray(scaled.reshape(k // 512, 128, 4, n).transpose(0, 1, 3, 2))
    if fmt == "e4m3":
        words = by_word.astype(ml_dtypes.float8_e4m3fn).view(np.uint8)
    else:
        c = by_word.astype(ml_dtypes.float4_e2m1fn).view(np.uint8) & 0xF
        words = (c[..., 0::2] | (c[..., 1::2] << 4)).reshape(k // 512, 128, 2 * n)
    return np.ascontiguousarray(words), np.ascontiguousarray(byte.astype(np.uint8).reshape(k // 512, 16, n))


def unpack_weight(words, scales, fmt):
    g, _, n = scales.shape
    words = np.ascontiguousarray(words).reshape(g, 128, n, -1)
    if fmt == "e4m3":
        vals = words.view(ml_dtypes.float8_e4m3fn).astype(np.float64)
    else:
        nib = np.empty((g, 128, n, 4), np.uint8)
        nib[..., 0::2] = words & 0xF
        nib[..., 1::2] = words >> 4
        vals = E2M1[nib]
    vals = vals * np.repeat(np.exp2(scales.astype(np.float64) - 127.0), 8, axis=1)[..., None]
    return vals.transpose(0, 1, 3, 2).reshape(g * 512, n)


def sigmoid(v):
    return 1.0 / (1.0 + np.exp(-v))


K, T, I, G, E = 512, 2048, 1024, 128, 512


def setup_inputs():
    n = np.random.standard_normal
    idx = np.random.permutation(T)[:I]
    fk = mx_kscale(K)
    nodep = pack_weight(n((K, T)) / fk[:, None], "e2m1")
    return {
        "node_words": nodep[0],
        "node_scales": nodep[1],
        "wg": (n((K, E)) * 1 / np.sqrt(K) * fk[:, None]).astype(np.float32),
        "wv": (n((K, E)) * 1 / np.sqrt(K) * fk[:, None]).astype(np.float32),
        "bg": (0.5 * n((E, 1))).astype(np.float32),
        "offs": striped(idx),
    }


def reference(node_words, node_scales, wg, wv, bg, offs):
    idx = unstriped(offs)
    nodeu = unpack_weight(node_words, node_scales, "e2m1")
    wgq = mxq(f64(wg), 0, "e4m3")
    nodeidxg = nodeu[:, idx]
    z = wgq.T @ nodeidxg
    wvq = mxq(f64(wv), 0, "e4m3")
    v = wvq.T @ nodeidxg
    x = sigmoid(z + f64(bg)) * np.tanh(v)
    y = x.reshape(E, G, I // G).sum(axis=2)
    return y

from contextlib import ExitStack

import concourse.mybir as mybir
from concourse.masks import make_identity

K, T, I, G, E = 512, 2048, 1024, 128, 512
FLOPS = 2 * 2 * K * E * I

F32 = mybir.dt.float32
BF16 = mybir.dt.bfloat16
I32 = mybir.dt.int32
U32 = mybir.dt.uint32
U16 = mybir.dt.uint16
U8 = mybir.dt.uint8
FP8X4 = mybir.dt.float8_e4m3fn_x4
FP4X4 = mybir.dt.float4_e2m1fn_x4
ACT = mybir.ActivationFunctionType
ALU = mybir.AluOpType
AX = mybir.AxisListType

P = 128
PACK = 4
HALF = 512
NODES = I // G
TILES = E // P
SCALAR_CASTS = 4


def tile_attend_gatedreadout_kernel(tc, node_words, node_scales, wg, wv, bg, offs, out):
    nc = tc.nc
    with ExitStack() as ctx:
        keep = ctx.enter_context(tc.tile_pool(name="keep", bufs=1))
        mm = ctx.enter_context(tc.psum_pool(name="mm", bufs=5))
        acc = ctx.enter_context(tc.psum_pool(name="acc", bufs=2))
        fin = ctx.enter_context(tc.psum_pool(name="fin", bufs=1))

        offsets = keep.tile([P, I // 16], U16, name="offsets")
        words = keep.tile([P, T], U16, name="words", align_bytes=64)
        scales = keep.tile([P, T], U8, name="scales", align_bytes=64)
        bias = keep.tile([P, TILES], F32, name="bias")
        ident = keep.tile([P, P], F32, name="ident", align_bytes=64)

        jobs = [(w, c) for c in range(TILES) for w in (0, 1)]
        mats = (wg, wv)
        raw = {}

        def load_w(job):
            w, c = job
            raw[job] = keep.tile([P, PACK, P], F32, name="raw%d%d" % job, align_bytes=64)
            nc.sync.dma_start(
                out=raw[job][:],
                in_=mats[w].rearrange("(p j) e -> p j e", j=PACK)[:, :, c * P : (c + 1) * P],
            )

        nc.gpsimd.memset(scales[:].bitcast(I32), 0)
        nc.sync.dma_start(offsets[:], offs)
        for q in range(4):
            nc.sync.dma_start(
                out=scales[32 * q : 32 * q + 4, :].bitcast(I32),
                in_=node_scales[0, 4 * q : 4 * q + 4, :].bitcast(I32),
            )
        nc.sync.dma_start(out=words[:].bitcast(I32), in_=node_words[0].bitcast(I32))
        load_w(jobs[0])
        load_w(jobs[1])
        with nc.allow_non_contiguous_dma(reason="one bias value a partition"):
            nc.sync.dma_start(out=bias[:], in_=bg.rearrange("(c p) o -> p (c o)", p=P))
        for job in jobs[2:]:
            load_w(job)
        make_identity(nc, ident[:])

        grouped, codes, planes = {}, {}, {}

        def cast(job, on_scalar):
            grouped[job] = keep.tile([P, P, PACK], BF16, name="grp%d%d" % job, tag="grp%d%d" % job, align_bytes=64)
            dst = grouped[job][:].rearrange("p (c i) t -> p c t i", i=4)
            src = raw[job][:].rearrange("p t (c i) -> p c t i", i=4)
            if on_scalar:
                nc.scalar.copy(out=dst, in_=src)
            else:
                nc.vector.tensor_copy(out=dst, in_=src)

        def quantize(job):
            codes[job] = keep.tile([P, P], U32, name="codes%d%d" % job, align_bytes=64)
            planes[job] = keep.tile([P, P], U8, name="plane%d%d" % job, align_bytes=64)
            nc.vector.quantize_mx(
                out=codes[job][:].bitcast(FP8X4),
                scales=planes[job][:],
                in_=grouped[job][:].rearrange("p c t -> p (c t)"),
            )

        gw, gs = {}, {}

        def gather_scales(h, tag):
            gs[h] = keep.tile([P, HALF], U8, name="gs%d" % h, tag=tag, align_bytes=64)
            nc.vector.tensor_copy(gs[h][:], scales[:].indirect(offsets[:, h * 32 : (h + 1) * 32]))

        def gather_words(h, tag):
            gw[h] = keep.tile([P, HALF], U16, name="gw%d" % h, tag=tag, align_bytes=64)
            nc.vector.tensor_copy(gw[h][:], words[:].indirect(offsets[:, h * 32 : (h + 1) * 32]))

        acts = {}

        def project(job, h):
            w, c = job
            bank = mm.tile([P, HALF], F32, name="bank")
            nc.tensor.matmul_mx(
                out=bank[:],
                lhsT=codes[job][:].bitcast(FP8X4),
                lhsT_scale=planes[job][:],
                rhs=gw[h][:].bitcast(FP4X4),
                rhs_scale=gs[h][:],
                start=True,
                stop=True,
            )
            acts[job, h] = keep.tile([P, HALF], F32, name="act%d%d%d" % (w, c, h), align_bytes=64)
            if c < TILES - 1:
                src = bank[:].rearrange("p (g j) -> p j g", j=NODES)
                dst = acts[job, h][:].rearrange("p (j g) -> p j g", j=NODES)
            else:
                src = bank[:]
                dst = acts[job, h][:]
            if w == 0:
                nc.scalar.activation(dst, src, ACT.Sigmoid, bias=bias[:, c : c + 1])
            else:
                nc.scalar.activation(dst, src, ACT.Tanh)

        prods = {}

        def product(c, h):
            if h == 0:
                prods[c] = keep.tile([P, I], F32, name="prod%d" % c, align_bytes=64)
            a, b = acts[(0, c), h], acts[(1, c), h]
            if c < TILES - 1:
                dst = prods[c][:].rearrange("p (j g) -> p j g", j=NODES)[:, :, h * 64 : (h + 1) * 64]
                nc.vector.tensor_tensor(
                    dst,
                    a[:].rearrange("p (j g) -> p j g", j=NODES),
                    b[:].rearrange("p (j g) -> p j g", j=NODES),
                    ALU.mult,
                )
            else:
                nc.vector.tensor_tensor(prods[c][:, h * HALF : (h + 1) * HALF], a[:], b[:], ALU.mult)

        def sum_on_tensor(c):
            turned = acc.tile([P, P], F32, name="turned")
            for j in range(NODES):
                nc.tensor.matmul(
                    turned[:],
                    lhsT=prods[c][:, j * P : (j + 1) * P],
                    rhs=ident[:],
                    is_transpose=True,
                    start=(j == 0),
                    stop=(j == NODES - 1),
                )
            staged = keep.tile([P, P], F32, name="staged%d" % c, align_bytes=64)
            nc.scalar.copy(out=staged[:], in_=turned[:])
            back = fin.tile([P, P], F32, name="back")
            nc.tensor.transpose(back[:], staged[:], ident[:])
            result = keep.tile([P, P], F32, name="result%d" % c, align_bytes=64)
            nc.vector.tensor_copy(out=result[:], in_=back[:])
            nc.sync.dma_start(out=out[c * P : (c + 1) * P, :], in_=result[:])

        def sum_on_vector(c, h):
            result = keep.tile([P, 64], F32, name="tail%d" % h, align_bytes=64)
            nc.vector.tensor_reduce(
                result[:],
                prods[c][:, h * HALF : (h + 1) * HALF].rearrange("p (g j) -> p g j", j=NODES),
                AX.X,
                ALU.add,
            )
            nc.sync.dma_start(out=out[c * P : (c + 1) * P, h * 64 : (h + 1) * 64], in_=result[:])

        gather_scales(0, "gs0")
        gather_words(0, "gw0")
        cast(jobs[0], True)
        cast(jobs[1], True)
        cast(jobs[2], True)
        quantize(jobs[0])
        gather_scales(1, "grp%d%d" % jobs[0])
        project(jobs[0], 0)
        quantize(jobs[1])
        quantize(jobs[2])
        cast(jobs[3], True)
        gather_words(1, "grp%d%d" % jobs[2])
        project(jobs[1], 0)
        project(jobs[2], 0)
        quantize(jobs[3])
        project(jobs[0], 1)
        project(jobs[1], 1)
        project(jobs[3], 0)
        for n in range(4, 8):
            cast(jobs[n], False)
            if n > 4:
                quantize(jobs[n - 1])
        product(0, 0)
        quantize(jobs[7])
        product(0, 1)
        project(jobs[2], 1)
        project(jobs[3], 1)
        product(1, 0)
        product(1, 1)
        for c in range(2, TILES):
            for h in range(2):
                project((0, c), h)
                project((1, c), h)
                product(c, h)
                if c == TILES - 1:
                    sum_on_vector(c, h)
                if h == 0:
                    sum_on_tensor(c - 2)
                if c == TILES - 1 and h == 0:
                    sum_on_tensor(c - 1)
